import numpy as np
import ml_dtypes


def mxq(x, axis, fmt="e4m3"):
    dtype, down = {"e4m3": (ml_dtypes.float8_e4m3fn, 7), "e5m2": (ml_dtypes.float8_e5m2, 14)}[fmt]
    v = np.moveaxis(np.asarray(x, np.float32).astype(ml_dtypes.bfloat16).astype(np.float64), axis, -1)
    blocks = v.reshape(v.shape[:-1] + (-1, 32))
    amax = np.abs(blocks).max(-1, keepdims=True)
    byte = np.maximum(np.where(amax > 0, np.frexp(amax)[1] - 1 + 127, 0) - down, 1)
    scale = np.exp2(byte - 127.0)
    codes = (blocks / scale).astype(np.float32).astype(dtype).astype(np.float64)
    return np.moveaxis((codes * scale).reshape(v.shape), -1, axis)


WIDE = False


def mx_kscale(k):
    if not WIDE:
        return np.ones(k)
    levels = np.array([10, -10, 5, -5, 0])
    if k % 512:
        return np.exp2(np.random.permutation(np.resize(levels, k // 32))).repeat(32)
    a = np.empty((k // 512, 16))
    for p in range(k // 512):
        a[p, :8] = np.random.permutation(np.resize(levels, 8))
        for g in range(8):
            far = levels[np.abs(levels - a[p, g]) >= 10]
            a[p, g + 8] = far[np.random.randint(len(far))]
    return np.exp2(a.ravel()).repeat(32)


def f64(x):
    return np.asarray(x).astype(np.float64)


def striped8(idx):
    return np.asarray(idx).reshape(8, -1, 16).transpose(0, 2, 1).reshape(128, -1).astype(np.uint16)


def unstriped8(offs):
    return offs.reshape(8, 16, -1).transpose(0, 2, 1).reshape(8, -1).astype(np.int64)


def pick8(x, idx, run):
    r = np.arange(len(x))
    return x[r[:, None], idx[r % (8 * run) // run]]


E2M1 = np.array([0.0, 0.5, 1.0, 1.5, 2.0, 3.0, 4.0, 6.0, -0.0, -0.5, -1.0, -1.5, -2.0, -3.0, -4.0, -6.0])


def pack_weight(w, fmt):
    k, n = w.shape
    w = f64(np.asarray(w, np.float32).astype(ml_dtypes.bfloat16)).reshape(k // 32, 32, n)
    amax = np.abs(w).max(1)
    if fmt == "e4m3":
        byte = np.frexp(amax)[1] - 1 + 127 - 7
    else:
        mant, ex = np.frexp(amax / 6.0)
        byte = np.where(mant > 0.5, ex, ex - 1) + 127
    byte = np.clip(np.where(amax > 0, byte, 1), 1, 254)
    scaled = (w * np.exp2(127.0 - byte)[:, None, :]).reshape(k, n).astype(np.float32)
    by_word = np.ascontiguousarray(scaled.reshape(k // 512, 128, 4, n).transpose(0, 1, 3, 2))
    if fmt == "e4m3":
        words = by_word.astype(ml_dtypes.float8_e4m3fn).view(np.uint8)
    else:
        c = by_word.astype(ml_dtypes.float4_e2m1fn).view(np.uint8) & 0xF
        words = (c[..., 0::2] | (c[..., 1::2] << 4)).reshape(k // 512, 128, 2 * n)
    return np.ascontiguousarray(words), np.ascontiguousarray(byte.astype(np.uint8).reshape(k // 512, 16, n))


def unpack_weight(words, scales, fmt):
    g, _, n = scales.shape
    words = np.ascontiguousarray(words).reshape(g, 128, n, -1)
    if fmt == "e4m3":
        vals = words.view(ml_dtypes.float8_e4m3fn).astype(np.float64)
    else:
        nib = np.empty((g, 128, n, 4), np.uint8)
        nib[..., 0::2] = words & 0xF
        nib[..., 1::2] = words >> 4
        vals = E2M1[nib]
    vals = vals * np.repeat(np.exp2(scales.astype(np.float64) - 127.0), 8, axis=1)[..., None]
    return vals.transpose(0, 1, 3, 2).reshape(g * 512, n)


D, T, U, I, Q = 512, 1024, 1024, 512, 128


def setup_inputs():
    n = np.random.standard_normal
    idx = np.stack([np.random.permutation(T)[:I] for _ in range(8)])
    idx2 = np.stack([np.random.permutation(T)[:I] for _ in range(8)])
    idx3 = np.stack([np.random.permutation(U)[:I] for _ in range(8)])
    idx4 = np.stack([np.random.permutation(T)[:I] for _ in range(8)])
    idx5 = np.stack([np.random.permutation(U)[:I] for _ in range(8)])
    fd = mx_kscale(D)
    keysp = pack_weight(n((D, T)) / fd[:, None], "e4m3")
    notesp = pack_weight(n((D, U)) / fd[:, None], "e2m1")
    return {
        "query": (n((D, Q)) * 1.0 / np.sqrt(D) * fd[:, None]).astype(np.float32),
        "keys_words": keysp[0],
        "keys_scales": keysp[1],
        "notes_words": notesp[0],
        "notes_scales": notesp[1],
        "offs": striped8(idx),
        "offs2": striped8(idx2),
        "offs3": striped8(idx3),
        "offs4": striped8(idx4),
        "offs5": striped8(idx5),
    }


def reference(query, keys_words, keys_scales, notes_words, notes_scales, offs, offs2, offs3, offs4, offs5):
    idx = unstriped8(offs)
    idx2 = unstriped8(offs2)
    idx3 = unstriped8(offs3)
    idx4 = unstriped8(offs4)
    idx5 = unstriped8(offs5)
    keysu = unpack_weight(keys_words, keys_scales, "e4m3")
    notesu = unpack_weight(notes_words, notes_scales, "e2m1")
    queryq = mxq(f64(query), 0, "e4m3")
    a = queryq.T @ keysu
    b = queryq.T @ notesu
    hi1 = np.maximum(pick8(a, idx, 16), pick8(a, idx2, 16))
    r = hi1 - pick8(b, idx3, 16)
    f1 = np.zeros((Q, T))
    f1[np.arange(Q)[:, None], idx4[np.arange(Q) % 128 // 16]] = r
    aa = a - f1
    v = np.minimum(pick8(aa, idx, 16), pick8(b, idx5, 16))
    y = v + r
    return y

@@ -1,0 +1,126 @@
+from contextlib import ExitStack
+
+import concourse.mybir as mybir
+
+D, T, U, I, Q = 512, 1024, 1024, 512, 128
+FLOPS = 2 * D * Q * (T + U)
+
+F32 = mybir.dt.float32
+BF16 = mybir.dt.bfloat16
+I32 = mybir.dt.int32
+U32 = mybir.dt.uint32
+U16 = mybir.dt.uint16
+U8 = mybir.dt.uint8
+FP8X4 = mybir.dt.float8_e4m3fn_x4
+FP4X4 = mybir.dt.float4_e2m1fn_x4
+ALU = mybir.AluOpType
+COPY = mybir.ActivationFunctionType.Copy
+
+P = 128
+PACK = 4
+N = 256
+HALF = I // 2
+HC = HALF // 16
+
+
+def tile_attend_outbid_two_kernel(tc, query, keys_words, keys_scales, notes_words, notes_scales,
+                                   offs, offs2, offs3, offs4, offs5, out):
+    nc = tc.nc
+    with ExitStack() as ctx:
+        lists = ctx.enter_context(tc.tile_pool(name="lists", bufs=1))
+        sb = ctx.enter_context(tc.tile_pool(name="sb", bufs=1))
+        psum = ctx.enter_context(tc.psum_pool(name="psum", bufs=1))
+
+        q_raw = sb.tile([P, PACK, Q], F32, name="q_raw")
+        k_words = sb.tile([P, T], U32, name="k_words", align_bytes=64)
+        k_scales = sb.tile([P, T], U8, name="k_scales", align_bytes=64)
+        n_words = sb.tile([P, 2 * U], U8, name="n_words", align_bytes=64)
+        n_scales = sb.tile([P, U], U8, name="n_scales", align_bytes=64)
+        idx = [lists.tile([P, I // 16], U16, name="idx%d" % j) for j in range(5)]
+
+        nc.sync.dma_start(out=q_raw[:], in_=query.rearrange("(p j) w -> p j w", j=PACK))
+        for g in range(4):
+            nc.sync.dma_start(out=k_scales[32 * g:32 * g + 4, :].bitcast(I32),
+                                in_=keys_scales[0, 4 * g:4 * g + 4, :].bitcast(I32))
+        nc.sync.dma_start(out=k_words[:].bitcast(I32),
+                          in_=keys_words[0].rearrange("p n t -> p (n t)").bitcast(I32))
+        nc.sync.dma_start(out=n_words[:].bitcast(I32), in_=notes_words[0].bitcast(I32))
+        for g in range(4):
+            nc.sync.dma_start(out=n_scales[32 * g:32 * g + 4, :].bitcast(I32),
+                                in_=notes_scales[0, 4 * g:4 * g + 4, :].bitcast(I32))
+        for tile, src in zip(idx, (offs, offs2, offs3, offs4, offs5)):
+            nc.sync.dma_start(tile[:], src)
+        i1, i2, i3, i4, i5 = idx
+
+        f1 = sb.tile([P, T], F32, name="f1")
+        nc.vector.memset(f1[:], 0.0)
+
+        q_bf = sb.tile([P, Q, PACK], BF16, name="q_bf", align_bytes=64)
+        nc.vector.tensor_copy(out=q_bf[:], in_=q_raw[:].rearrange("p j w -> p w j"))
+        q_codes = sb.tile([P, Q], U32, name="q_codes", align_bytes=64)
+        q_scales = sb.tile([P, Q], U8, name="q_scales", align_bytes=64)
+        nc.vector.quantize_mx(out=q_codes[:].bitcast(FP8X4), scales=q_scales[:],
+                              in_=q_bf[:].rearrange("p w j -> p (w j)"))
+
+        a = sb.tile([P, T], F32, name="a", tag="a")
+        b = sb.tile([P, U], F32, name="b")
+        for j in range(T // N):
+            cols = slice(j * N, (j + 1) * N)
+            acc = psum.tile([P, N], F32, name="acc_a%d" % j)
+            nc.tensor.matmul_mx(out=acc[:], lhsT=q_codes[:].bitcast(FP8X4), lhsT_scale=q_scales[:],
+                                rhs=k_words[:, cols].bitcast(FP8X4), rhs_scale=k_scales[:, cols],
+                                start=True, stop=True)
+            if j % 2 == 0:
+                nc.scalar.copy(out=a[:, cols], in_=acc[:])
+            else:
+                nc.vector.tensor_copy(out=a[:, cols], in_=acc[:])
+        for j in range(U // N):
+            cols = slice(j * N, (j + 1) * N)
+            acc = psum.tile([P, N], F32, name="acc_b%d" % j)
+            nc.tensor.matmul_mx(out=acc[:], lhsT=q_codes[:].bitcast(FP8X4), lhsT_scale=q_scales[:],
+                                rhs=n_words[:, 2 * j * N:2 * (j + 1) * N].bitcast(FP4X4),
+                                rhs_scale=n_scales[:, cols], start=True, stop=True)
+            nc.scalar.copy(out=b[:, cols], in_=acc[:])
+
+        def half(name, h):
+            return sb.tile([P, HALF], F32, name="%s%d" % (name, h))
+
+        def part(lst, h):
+            return lst[:, h * HC:(h + 1) * HC]
+
+        early = sb.tile([P, 2, HALF], F32, name="early", tag="picked")
+        nb3_0 = half("nb3_", 0)
+        hi = [half("hi_", h) for h in range(2)]
+        r1 = half("r_", 1)
+
+        nc.vector.tensor_copy(early[:, 0, :], a[:].indirect(part(i1, 0)))
+        nc.vector.tensor_copy(early[:, 1, :], a[:].indirect(part(i2, 0)))
+        nc.scalar.activation(nb3_0[:], b[:].indirect(part(i3, 0)), COPY, scale=-1.0)
+        nc.vector.tensor_tensor(hi[0][:], early[:, 0, :], early[:, 1, :], ALU.max)
+        late = sb.tile([P, 5, HALF], F32, name="late", tag="picked")
+        nb3 = [nb3_0[:], late[:, 2, :]]
+        b5 = [late[:, 3, :], late[:, 4, :]]
+        nc.scalar.activation(late[:, 0, :], a[:].indirect(part(i1, 1)), COPY)
+        nc.scalar.activation(late[:, 1, :], a[:].indirect(part(i2, 1)), COPY)
+        nc.scalar.activation(nb3[1], b[:].indirect(part(i3, 1)), COPY, scale=-1.0)
+        nc.vector.tensor_tensor(f1[:].indirect(part(i4, 0)), hi[0][:], nb3[0], ALU.add)
+        nc.vector.tensor_tensor(hi[1][:], late[:, 0, :], late[:, 1, :], ALU.max)
+        nc.vector.tensor_tensor(f1[:].indirect(part(i4, 1)), hi[1][:], nb3[1], ALU.add)
+        nc.scalar.activation(late[:, 3:5, :].rearrange("p h n -> p (h n)"), b[:].indirect(i5[:]), COPY)
+        nc.vector.tensor_tensor(r1[:], hi[1][:], nb3[1], ALU.add)
+
+        aa = sb.tile([P, T], F32, name="aa")
+        nc.vector.tensor_tensor(aa[:], a[:], f1[:], ALU.subtract)
+        g = [half("g_", h) for h in range(2)]
+        v = [half("v_", h) for h in range(2)]
+        y = [half("y_", h) for h in range(2)]
+        nc.vector.tensor_copy(g[0][:], aa[:].indirect(part(i1, 0)))
+        nc.scalar.activation(g[1][:], aa[:].indirect(part(i1, 1)), COPY)
+        r0 = sb.tile([P, HALF], F32, name="r0", tag="a")
+        nc.vector.tensor_tensor(r0[:], hi[0][:], nb3[0], ALU.add)
+        r = [r0, r1]
+        for h in range(2):
+            nc.vector.tensor_tensor(v[h][:], g[h][:], b5[h], ALU.min)
+        for h in range(2):
+            nc.vector.tensor_tensor(y[h][:], v[h][:], r[h][:], ALU.add)
+            nc.sync.dma_start(out=out[:, h * HALF:(h + 1) * HALF], in_=y[h][:])

@@ -32,7 +32,7 @@ def tile_attend_outbid_two_kernel(tc, query, keys_words, keys_scales, notes_word
         psum = ctx.enter_context(tc.psum_pool(name="psum", bufs=1))
 
         q_raw = sb.tile([P, PACK, Q], F32, name="q_raw")
-        k_words = sb.tile([P, T], U32, name="k_words", align_bytes=64)
+        k_words = [sb.tile([P, T // 2], U32, name="k_words%d" % s, align_bytes=64) for s in range(2)]
         k_scales = sb.tile([P, T], U8, name="k_scales", align_bytes=64)
         n_words = sb.tile([P, 2 * U], U8, name="n_words", align_bytes=64)
         n_scales = sb.tile([P, U], U8, name="n_scales", align_bytes=64)
@@ -42,8 +42,9 @@ def tile_attend_outbid_two_kernel(tc, query, keys_words, keys_scales, notes_word
         for g in range(4):
             nc.sync.dma_start(out=k_scales[32 * g:32 * g + 4, :].bitcast(I32),
                                 in_=keys_scales[0, 4 * g:4 * g + 4, :].bitcast(I32))
-        nc.sync.dma_start(out=k_words[:].bitcast(I32),
-                          in_=keys_words[0].rearrange("p n t -> p (n t)").bitcast(I32))
+        for s in range(2):
+            nc.sync.dma_start(out=k_words[s][:].bitcast(I32),
+                              in_=keys_words[0, :, s * (T // 2):(s + 1) * (T // 2), :].rearrange("p n t -> p (n t)").bitcast(I32))
         nc.sync.dma_start(out=n_words[:].bitcast(I32), in_=notes_words[0].bitcast(I32))
         for g in range(4):
             nc.sync.dma_start(out=n_scales[32 * g:32 * g + 4, :].bitcast(I32),
@@ -56,7 +57,8 @@ def tile_attend_outbid_two_kernel(tc, query, keys_words, keys_scales, notes_word
         nc.vector.memset(f1[:], 0.0)
 
         q_bf = sb.tile([P, Q, PACK], BF16, name="q_bf", align_bytes=64)
-        nc.vector.tensor_copy(out=q_bf[:], in_=q_raw[:].rearrange("p j w -> p w j"))
+        nc.vector.tensor_copy(out=q_bf[:, 0:Q // 2, :], in_=q_raw[:, :, 0:Q // 2].rearrange("p j w -> p w j"))
+        nc.scalar.copy(out=q_bf[:, Q // 2:Q, :], in_=q_raw[:, :, Q // 2:Q].rearrange("p j w -> p w j"))
         q_codes = sb.tile([P, Q], U32, name="q_codes", align_bytes=64)
         q_scales = sb.tile([P, Q], U8, name="q_scales", align_bytes=64)
         nc.vector.quantize_mx(out=q_codes[:].bitcast(FP8X4), scales=q_scales[:],
@@ -64,12 +66,14 @@ def tile_attend_outbid_two_kernel(tc, query, keys_words, keys_scales, notes_word
 
         a = sb.tile([P, T], F32, name="a", tag="a")
         b = sb.tile([P, U], F32, name="b")
+        a_banks = []
         for j in range(T // N):
             cols = slice(j * N, (j + 1) * N)
             acc = psum.tile([P, N], F32, name="acc_a%d" % j)
             nc.tensor.matmul_mx(out=acc[:], lhsT=q_codes[:].bitcast(FP8X4), lhsT_scale=q_scales[:],
-                                rhs=k_words[:, cols].bitcast(FP8X4), rhs_scale=k_scales[:, cols],
+                                rhs=k_words[j // 2][:, (j % 2) * N:(j % 2 + 1) * N].bitcast(FP8X4), rhs_scale=k_scales[:, cols],
                                 start=True, stop=True)
+            a_banks.append(acc)
             if j % 2 == 0:
                 nc.scalar.copy(out=a[:, cols], in_=acc[:])
             else:
@@ -105,22 +109,24 @@ def tile_attend_outbid_two_kernel(tc, query, keys_words, keys_scales, notes_word
         nc.scalar.activation(nb3[1], b[:].indirect(part(i3, 1)), COPY, scale=-1.0)
         nc.vector.tensor_tensor(f1[:].indirect(part(i4, 0)), hi[0][:], nb3[0], ALU.add)
         nc.vector.tensor_tensor(hi[1][:], late[:, 0, :], late[:, 1, :], ALU.max)
+        r0 = sb.tile([P, HALF], F32, name="r0", tag="a")
+        nc.vector.tensor_tensor(r0[:], hi[0][:], nb3[0], ALU.add)
         nc.vector.tensor_tensor(f1[:].indirect(part(i4, 1)), hi[1][:], nb3[1], ALU.add)
-        nc.scalar.activation(late[:, 3:5, :].rearrange("p h n -> p (h n)"), b[:].indirect(i5[:]), COPY)
+        for h in (1, 0):
+            nc.scalar.activation(b5[h], b[:].indirect(part(i5, h)), COPY)
         nc.vector.tensor_tensor(r1[:], hi[1][:], nb3[1], ALU.add)
 
         aa = sb.tile([P, T], F32, name="aa")
-        nc.vector.tensor_tensor(aa[:], a[:], f1[:], ALU.subtract)
-        g = [half("g_", h) for h in range(2)]
-        v = [half("v_", h) for h in range(2)]
+        for j in range(T // N):
+            cols = slice(j * N, (j + 1) * N)
+            nc.vector.tensor_tensor(aa[:, cols], a_banks[j][:], f1[:, cols], ALU.subtract)
+        c0, t0, g1, v1 = half("c", 0), half("t", 0), half("g", 1), half("v", 1)
         y = [half("y_", h) for h in range(2)]
-        nc.vector.tensor_copy(g[0][:], aa[:].indirect(part(i1, 0)))
-        nc.scalar.activation(g[1][:], aa[:].indirect(part(i1, 1)), COPY)
-        r0 = sb.tile([P, HALF], F32, name="r0", tag="a")
-        nc.vector.tensor_tensor(r0[:], hi[0][:], nb3[0], ALU.add)
-        r = [r0, r1]
-        for h in range(2):
-            nc.vector.tensor_tensor(v[h][:], g[h][:], b5[h], ALU.min)
-        for h in range(2):
-            nc.vector.tensor_tensor(y[h][:], v[h][:], r[h][:], ALU.add)
-            nc.sync.dma_start(out=out[:, h * HALF:(h + 1) * HALF], in_=y[h][:])
+        nc.vector.tensor_tensor(t0[:], aa[:].indirect(part(i1, 0)), r0[:], ALU.add)
+        nc.scalar.activation(g1[:], aa[:].indirect(part(i1, 1)), COPY)
+        nc.vector.tensor_tensor(c0[:], b5[0], r0[:], ALU.add)
+        nc.vector.tensor_tensor(v1[:], g1[:], b5[1], ALU.min)
+        nc.vector.tensor_tensor(y[0][:], t0[:], c0[:], ALU.min)
+        nc.sync.dma_start(out=out[:, 0:HALF], in_=y[0][:])
+        nc.vector.tensor_tensor(y[1][:], v1[:], r1[:], ALU.add)
+        nc.sync.dma_start(out=out[:, HALF:I], in_=y[1][:])

@@ -34,7 +34,7 @@ def tile_attend_outbid_two_kernel(tc, query, keys_words, keys_scales, notes_word
         q_raw = sb.tile([P, PACK, Q], F32, name="q_raw")
         k_words = [sb.tile([P, T // 2], U32, name="k_words%d" % s, align_bytes=64) for s in range(2)]
         k_scales = sb.tile([P, T], U8, name="k_scales", align_bytes=64)
-        n_words = sb.tile([P, 2 * U], U8, name="n_words", align_bytes=64)
+        n_words = [sb.tile([P, U], U8, name="n_words%d" % s, align_bytes=64) for s in range(2)]
         n_scales = sb.tile([P, U], U8, name="n_scales", align_bytes=64)
         idx = [lists.tile([P, I // 16], U16, name="idx%d" % j) for j in range(5)]
 
@@ -45,10 +45,11 @@ def tile_attend_outbid_two_kernel(tc, query, keys_words, keys_scales, notes_word
         for s in range(2):
             nc.sync.dma_start(out=k_words[s][:].bitcast(I32),
                               in_=keys_words[0, :, s * (T // 2):(s + 1) * (T // 2), :].rearrange("p n t -> p (n t)").bitcast(I32))
-        nc.sync.dma_start(out=n_words[:].bitcast(I32), in_=notes_words[0].bitcast(I32))
+        nc.sync.dma_start(out=n_words[0][:].bitcast(I32), in_=notes_words[0, :, 0:U].bitcast(I32))
         for g in range(4):
             nc.sync.dma_start(out=n_scales[32 * g:32 * g + 4, :].bitcast(I32),
                                 in_=notes_scales[0, 4 * g:4 * g + 4, :].bitcast(I32))
+        nc.sync.dma_start(out=n_words[1][:].bitcast(I32), in_=notes_words[0, :, U:2 * U].bitcast(I32))
         for tile, src in zip(idx, (offs, offs2, offs3, offs4, offs5)):
             nc.sync.dma_start(tile[:], src)
         i1, i2, i3, i4, i5 = idx
@@ -82,7 +83,7 @@ def tile_attend_outbid_two_kernel(tc, query, keys_words, keys_scales, notes_word
             cols = slice(j * N, (j + 1) * N)
             acc = psum.tile([P, N], F32, name="acc_b%d" % j)
             nc.tensor.matmul_mx(out=acc[:], lhsT=q_codes[:].bitcast(FP8X4), lhsT_scale=q_scales[:],
-                                rhs=n_words[:, 2 * j * N:2 * (j + 1) * N].bitcast(FP4X4),
+                                rhs=n_words[j // 2][:, 2 * (j % 2) * N:2 * (j % 2 + 1) * N].bitcast(FP4X4),
                                 rhs_scale=n_scales[:, cols], start=True, stop=True)
             nc.scalar.copy(out=b[:, cols], in_=acc[:])
 
@@ -101,7 +102,7 @@ def tile_attend_outbid_two_kernel(tc, query, keys_words, keys_scales, notes_word
         nc.vector.tensor_copy(early[:, 1, :], a[:].indirect(part(i2, 0)))
         nc.scalar.activation(nb3_0[:], b[:].indirect(part(i3, 0)), COPY, scale=-1.0)
         nc.vector.tensor_tensor(hi[0][:], early[:, 0, :], early[:, 1, :], ALU.max)
-        late = sb.tile([P, 5, HALF], F32, name="late", tag="picked")
+        late = sb.tile([P, 6, HALF], F32, name="late", tag="picked")
         nb3 = [nb3_0[:], late[:, 2, :]]
         b5 = [late[:, 3, :], late[:, 4, :]]
         nc.scalar.activation(late[:, 0, :], a[:].indirect(part(i1, 1)), COPY)
@@ -114,10 +115,12 @@ def tile_attend_outbid_two_kernel(tc, query, keys_words, keys_scales, notes_word
         nc.vector.tensor_tensor(f1[:].indirect(part(i4, 1)), hi[1][:], nb3[1], ALU.add)
         for h in (1, 0):
             nc.scalar.activation(b5[h], b[:].indirect(part(i5, h)), COPY)
+        nc.scalar.copy(out=late[:, 5, :], in_=a_banks[-1][:])
         nc.vector.tensor_tensor(r1[:], hi[1][:], nb3[1], ALU.add)
 
         aa = sb.tile([P, T], F32, name="aa")
-        for j in range(T // N):
+        nc.gpsimd.tensor_tensor(aa[:, T - N:T], late[:, 5, :], f1[:, T - N:T], ALU.subtract)
+        for j in range(T // N - 1):
             cols = slice(j * N, (j + 1) * N)
             nc.vector.tensor_tensor(aa[:, cols], a_banks[j][:], f1[:, cols], ALU.subtract)
         c0, t0, g1, v1 = half("c", 0), half("t", 0), half("g", 1), half("v", 1)

@@ -33,22 +33,22 @@ def tile_attend_outbid_two_kernel(tc, query, keys_words, keys_scales, notes_word
 
         q_raw = sb.tile([P, PACK, Q], F32, name="q_raw")
         k_words = [sb.tile([P, T // 2], U32, name="k_words%d" % s, align_bytes=64) for s in range(2)]
-        k_scales = sb.tile([P, T], U8, name="k_scales", align_bytes=64)
+        k_scales = sb.tile([P, N], U8, name="k_scales", align_bytes=64)
         n_words = [sb.tile([P, U], U8, name="n_words%d" % s, align_bytes=64) for s in range(2)]
         n_scales = sb.tile([P, U], U8, name="n_scales", align_bytes=64)
         idx = [lists.tile([P, I // 16], U16, name="idx%d" % j) for j in range(5)]
 
         nc.sync.dma_start(out=q_raw[:], in_=query.rearrange("(p j) w -> p j w", j=PACK))
         for g in range(4):
-            nc.sync.dma_start(out=k_scales[32 * g:32 * g + 4, :].bitcast(I32),
-                                in_=keys_scales[0, 4 * g:4 * g + 4, :].bitcast(I32))
+            nc.sync.dma_start(out=k_scales[32 * g:32 * g + 16, :].bitcast(I32),
+                              in_=keys_scales[0, 4 * g:4 * g + 4, :].bitcast(I32).rearrange("f (c n) -> c f n", c=4))
         for s in range(2):
             nc.sync.dma_start(out=k_words[s][:].bitcast(I32),
                               in_=keys_words[0, :, s * (T // 2):(s + 1) * (T // 2), :].rearrange("p n t -> p (n t)").bitcast(I32))
         nc.sync.dma_start(out=n_words[0][:].bitcast(I32), in_=notes_words[0, :, 0:U].bitcast(I32))
         for g in range(4):
-            nc.sync.dma_start(out=n_scales[32 * g:32 * g + 4, :].bitcast(I32),
-                                in_=notes_scales[0, 4 * g:4 * g + 4, :].bitcast(I32))
+            nc.sync.dma_start(out=n_scales[g:P:32, :].bitcast(I32),
+                                in_=notes_scales[0, g:16:4, :].bitcast(I32))
         nc.sync.dma_start(out=n_words[1][:].bitcast(I32), in_=notes_words[0, :, U:2 * U].bitcast(I32))
         for tile, src in zip(idx, (offs, offs2, offs3, offs4, offs5)):
             nc.sync.dma_start(tile[:], src)
@@ -72,7 +72,7 @@ def tile_attend_outbid_two_kernel(tc, query, keys_words, keys_scales, notes_word
             cols = slice(j * N, (j + 1) * N)
             acc = psum.tile([P, N], F32, name="acc_a%d" % j)
             nc.tensor.matmul_mx(out=acc[:], lhsT=q_codes[:].bitcast(FP8X4), lhsT_scale=q_scales[:],
-                                rhs=k_words[j // 2][:, (j % 2) * N:(j % 2 + 1) * N].bitcast(FP8X4), rhs_scale=k_scales[:, cols],
+                                rhs=k_words[j // 2][:, (j % 2) * N:(j % 2 + 1) * N].bitcast(FP8X4), rhs_scale=k_scales[4 * j:P, :],
                                 start=True, stop=True)
             a_banks.append(acc)
             if j % 2 == 0:

from contextlib import ExitStack

import concourse.mybir as mybir

D, T, U, I, Q = 512, 1024, 1024, 512, 128
FLOPS = 2 * D * Q * (T + U)

F32 = mybir.dt.float32
BF16 = mybir.dt.bfloat16
I32 = mybir.dt.int32
U32 = mybir.dt.uint32
U16 = mybir.dt.uint16
U8 = mybir.dt.uint8
FP8X4 = mybir.dt.float8_e4m3fn_x4
FP4X4 = mybir.dt.float4_e2m1fn_x4
ALU = mybir.AluOpType
COPY = mybir.ActivationFunctionType.Copy

P = 128
PACK = 4
N = 256
HALF = I // 2
HC = HALF // 16


def tile_attend_outbid_two_kernel(tc, query, keys_words, keys_scales, notes_words, notes_scales,
                                   offs, offs2, offs3, offs4, offs5, out):
    nc = tc.nc
    with ExitStack() as ctx:
        lists = ctx.enter_context(tc.tile_pool(name="lists", bufs=1))
        sb = ctx.enter_context(tc.tile_pool(name="sb", bufs=1))
        psum = ctx.enter_context(tc.psum_pool(name="psum", bufs=1))

        q_raw = sb.tile([P, PACK, Q], F32, name="q_raw")
        k_words = [sb.tile([P, T // 2], U32, name="k_words%d" % s, align_bytes=64) for s in range(2)]
        k_scales = sb.tile([P, N], U8, name="k_scales", align_bytes=64)
        n_words = [sb.tile([P, U], U8, name="n_words%d" % s, align_bytes=64) for s in range(2)]
        n_scales = sb.tile([P, U], U8, name="n_scales", align_bytes=64)
        idx = [lists.tile([P, I // 16], U16, name="idx%d" % j) for j in range(5)]

        nc.sync.dma_start(out=q_raw[:], in_=query.rearrange("(p j) w -> p j w", j=PACK))
        for g in range(4):
            nc.sync.dma_start(out=k_scales[32 * g:32 * g + 16, :].bitcast(I32),
                              in_=keys_scales[0, 4 * g:4 * g + 4, :].bitcast(I32).rearrange("f (c n) -> c f n", c=4))
        for s in range(2):
            nc.sync.dma_start(out=k_words[s][:].bitcast(I32),
                              in_=keys_words[0, :, s * (T // 2):(s + 1) * (T // 2), :].rearrange("p n t -> p (n t)").bitcast(I32))
        nc.sync.dma_start(out=n_words[0][:].bitcast(I32), in_=notes_words[0, :, 0:U].bitcast(I32))
        for g in range(4):
            nc.sync.dma_start(out=n_scales[g:P:32, :].bitcast(I32),
                                in_=notes_scales[0, g:16:4, :].bitcast(I32))
        nc.sync.dma_start(out=n_words[1][:].bitcast(I32), in_=notes_words[0, :, U:2 * U].bitcast(I32))
        for tile, src in zip(idx, (offs, offs2, offs3, offs4, offs5)):
            nc.sync.dma_start(tile[:], src)
        i1, i2, i3, i4, i5 = idx

        f1 = sb.tile([P, T], F32, name="f1")
        nc.vector.memset(f1[:], 0.0)

        q_bf = sb.tile([P, Q, PACK], BF16, name="q_bf", align_bytes=64)
        nc.vector.tensor_copy(out=q_bf[:, 0:Q // 2, :], in_=q_raw[:, :, 0:Q // 2].rearrange("p j w -> p w j"))
        nc.scalar.copy(out=q_bf[:, Q // 2:Q, :], in_=q_raw[:, :, Q // 2:Q].rearrange("p j w -> p w j"))
        q_codes = sb.tile([P, Q], U32, name="q_codes", align_bytes=64)
        q_scales = sb.tile([P, Q], U8, name="q_scales", align_bytes=64)
        nc.vector.quantize_mx(out=q_codes[:].bitcast(FP8X4), scales=q_scales[:],
                              in_=q_bf[:].rearrange("p w j -> p (w j)"))

        a = sb.tile([P, T], F32, name="a", tag="a")
        b = sb.tile([P, U], F32, name="b")
        a_banks = []
        for j in range(T // N):
            cols = slice(j * N, (j + 1) * N)
            acc = psum.tile([P, N], F32, name="acc_a%d" % j)
            nc.tensor.matmul_mx(out=acc[:], lhsT=q_codes[:].bitcast(FP8X4), lhsT_scale=q_scales[:],
                                rhs=k_words[j // 2][:, (j % 2) * N:(j % 2 + 1) * N].bitcast(FP8X4), rhs_scale=k_scales[4 * j:P, :],
                                start=True, stop=True)
            a_banks.append(acc)
            if j % 2 == 0:
                nc.scalar.copy(out=a[:, cols], in_=acc[:])
            else:
                nc.vector.tensor_copy(out=a[:, cols], in_=acc[:])
        for j in range(U // N):
            cols = slice(j * N, (j + 1) * N)
            acc = psum.tile([P, N], F32, name="acc_b%d" % j)
            nc.tensor.matmul_mx(out=acc[:], lhsT=q_codes[:].bitcast(FP8X4), lhsT_scale=q_scales[:],
                                rhs=n_words[j // 2][:, 2 * (j % 2) * N:2 * (j % 2 + 1) * N].bitcast(FP4X4),
                                rhs_scale=n_scales[:, cols], start=True, stop=True)
            nc.scalar.copy(out=b[:, cols], in_=acc[:])

        def half(name, h):
            return sb.tile([P, HALF], F32, name="%s%d" % (name, h))

        def part(lst, h):
            return lst[:, h * HC:(h + 1) * HC]

        early = sb.tile([P, 2, HALF], F32, name="early", tag="picked")
        nb3_0 = half("nb3_", 0)
        hi = [half("hi_", h) for h in range(2)]
        r1 = half("r_", 1)

        nc.vector.tensor_copy(early[:, 0, :], a[:].indirect(part(i1, 0)))
        nc.vector.tensor_copy(early[:, 1, :], a[:].indirect(part(i2, 0)))
        nc.scalar.activation(nb3_0[:], b[:].indirect(part(i3, 0)), COPY, scale=-1.0)
        nc.vector.tensor_tensor(hi[0][:], early[:, 0, :], early[:, 1, :], ALU.max)
        late = sb.tile([P, 6, HALF], F32, name="late", tag="picked")
        nb3 = [nb3_0[:], late[:, 2, :]]
        b5 = [late[:, 3, :], late[:, 4, :]]
        nc.scalar.activation(late[:, 0, :], a[:].indirect(part(i1, 1)), COPY)
        nc.scalar.activation(late[:, 1, :], a[:].indirect(part(i2, 1)), COPY)
        nc.scalar.activation(nb3[1], b[:].indirect(part(i3, 1)), COPY, scale=-1.0)
        nc.vector.tensor_tensor(f1[:].indirect(part(i4, 0)), hi[0][:], nb3[0], ALU.add)
        nc.vector.tensor_tensor(hi[1][:], late[:, 0, :], late[:, 1, :], ALU.max)
        r0 = sb.tile([P, HALF], F32, name="r0", tag="a")
        nc.vector.tensor_tensor(r0[:], hi[0][:], nb3[0], ALU.add)
        nc.vector.tensor_tensor(f1[:].indirect(part(i4, 1)), hi[1][:], nb3[1], ALU.add)
        for h in (1, 0):
            nc.scalar.activation(b5[h], b[:].indirect(part(i5, h)), COPY)
        nc.scalar.copy(out=late[:, 5, :], in_=a_banks[-1][:])
        nc.vector.tensor_tensor(r1[:], hi[1][:], nb3[1], ALU.add)

        aa = sb.tile([P, T], F32, name="aa")
        nc.gpsimd.tensor_tensor(aa[:, T - N:T], late[:, 5, :], f1[:, T - N:T], ALU.subtract)
        for j in range(T // N - 1):
            cols = slice(j * N, (j + 1) * N)
            nc.vector.tensor_tensor(aa[:, cols], a_banks[j][:], f1[:, cols], ALU.subtract)
        c0, t0, g1, v1 = half("c", 0), half("t", 0), half("g", 1), half("v", 1)
        y = [half("y_", h) for h in range(2)]
        nc.vector.tensor_tensor(t0[:], aa[:].indirect(part(i1, 0)), r0[:], ALU.add)
        nc.scalar.activation(g1[:], aa[:].indirect(part(i1, 1)), COPY)
        nc.vector.tensor_tensor(c0[:], b5[0], r0[:], ALU.add)
        nc.vector.tensor_tensor(v1[:], g1[:], b5[1], ALU.min)
        nc.vector.tensor_tensor(y[0][:], t0[:], c0[:], ALU.min)
        nc.sync.dma_start(out=out[:, 0:HALF], in_=y[0][:])
        nc.vector.tensor_tensor(y[1][:], v1[:], r1[:], ALU.add)
        nc.sync.dma_start(out=out[:, HALF:I], in_=y[1][:])
